import numpy as np
CORES = [97,101,225,229,353,357,481,485]
N = 8
W = 64
def setup_inputs(rng):
    amp = 0.5 + 1.5 * rng.random((2, N, 128, 1), dtype=np.float32)
    return {"u": amp[0] * rng.standard_normal((N, 128, W), dtype=np.float32), "b": amp[1] * rng.standard_normal((N, 128, W), dtype=np.float32)}
def setup_inputs_big(rng):
    d = setup_inputs(rng)
    for k in ("u", "b"): d[k] = (d[k].astype(np.float32) * 1024.0).astype(d[k].dtype)
    return d
def setup_inputs_small(rng):
    d = setup_inputs(rng)
    for k in ("u", "b"): d[k] = (d[k].astype(np.float32) * (1 / 1024.0)).astype(d[k].dtype)
    return d
def setup_inputs_apart(rng):
    d = setup_inputs(rng)
    f = (10.0 ** rng.permutation(np.linspace(-1.5, 1.5, N))).astype(np.float32).reshape(N, 1, 1)
    for k in ("u", "b"): d[k] = (d[k].astype(np.float32) * f).astype(d[k].dtype)
    return d
def reference(u, b):
    g = np.concatenate(list(u.astype(np.float64)), axis=1); bb = np.concatenate(list(b.astype(np.float64)), axis=1)
    p = np.concatenate([g[:, -2:], g, g[:, :2]], axis=1)
    n = 0.125 * (p[:, :-4] + p[:, 1:-3] + p[:, 3:-1] + p[:, 4:]) + 0.5 * bb
    d = n - g
    s = np.stack([(d ** 2).mean(axis=1), np.abs(d).max(axis=1)], axis=1)
    return {"y": np.stack([n[:, W * r:W * r + W] for r in range(N)]).astype(np.float32), "s": np.broadcast_to(s.astype(np.float32), (N, 128, 2))}

@@ -1,0 +1,219 @@
+from concourse.bass import DstId, RemoteDMATransfer
+from concourse.mybir import AluOpType
+
+F = "float32"
+SCRATCH = {
+    "U": ("sbuf", [128, 64], F), "Bb": ("sbuf", [128, 64], F),
+    "U8": ("sbuf", [128, 72], F), "A": ("sbuf", [128, 72], F), "Dx": ("sbuf", [128, 68], F),
+    "AB": ("sbuf", [128, 64], F), "NQ": ("sbuf", [128, 64], F), "TS": ("sbuf", [128, 64], F), "TM": ("sbuf", [128, 64], F),
+    "GR": ("sbuf", [128, 16], F), "GL": ("sbuf", [128, 16], F), "E": ("sbuf", [128, 16], F),
+    "AE": ("sbuf", [128, 16], F), "QE": ("sbuf", [128, 16], F), "Q8": ("sbuf", [128, 8], F), "A8": ("sbuf", [128, 8], F),
+    "SB": ("sbuf", [128, 32], F), "CA": ("sbuf", [128, 32], F), "RKO": ("sbuf", [128, 36], F),
+    "Y": ("sbuf", [128, 64], F), "OT": ("sbuf", [128, 16], F), "FT": ("sbuf", [128, 32], F),
+    "SS": ("sbuf", [128, 4], F), "SO": ("sbuf", [128, 4], F),
+    "PC": ("psum", [128, 256], F), "PW": ("psum", [128, 512], F),
+}
+SEMAPHORES = ["ldu", "ldb", "v", "pk", "pi", "fin", "sent", "st"]
+
+
+def _bits(m):
+    return [1 << i for i in range(m.bit_length()) if (m >> i) & 1]
+
+
+def _plan(T, topo):
+    cores = list(T.cores)
+    n = len(cores)
+
+    def rack(r):
+        return topo.rack(topo.host(cores[r]))
+
+    def window(x):
+        mem = [q for q in range(n) if rack(q) == rack(x)]
+        start = [q for q in mem if (q - 1) % n not in mem][0]
+        run = [(start + i) % n for i in range(len(mem))]
+        prev, nxt = (start - 1) % n, (run[-1] + 1) % n
+        if topo.may_write(cores[prev], cores[x]):
+            return [prev] + run, 0, run
+        return run + [nxt], len(run) - 1, run
+
+    def partner(x, same_rack):
+        return [y for y in range(n) if topo.host(cores[y]) != topo.host(cores[x]) and (rack(y) == rack(x)) == same_rack
+                and topo.may_write(cores[x], cores[y]) and topo.die(cores[y]) == topo.die(cores[x])][0]
+
+    def on_chip(a, b):
+        return topo.host(cores[a]) == topo.host(cores[b]) and topo.chip(cores[a]) == topo.chip(cores[b])
+
+    return cores, n, window, partner, on_chip
+
+
+def rank_program(g, core, T, topo):
+    x = T.rank_of(core)
+    if x is None:
+        return
+    cores, n, window, partner, on_chip = _plan(T, topo)
+    S, V = T.sem, g.vector
+    ADD, SUB, MUL, MAX = AluOpType.add, AluOpType.subtract, AluOpType.mult, AluOpType.max
+    win, ix, run = window(x)
+    p = win.index(x)
+    cable, rackp = partner(x, False), partner(x, True)
+    jx = window(rackp)[1]
+
+    def dst_id(r):
+        rid, pid = topo.addr(cores[r], core)
+        return DstId(rid=rid, pnc=pid)
+
+    peer = [r for r in range(n) if r != x and on_chip(r, x)][0]
+    low = _bits(topo.mask(core, cores[cable]))
+    high = [e for e in _bits(topo.mask(core, cores[peer])) if e not in low][:4]
+    h = len(low) // 2
+    lowA, lowB = sum(low[:h]), sum(low[h:])
+    nlow, npk = h, len(high) // 2
+
+    g.sync.dma_start(out=T.U[:, :], in_=T.u[:, :]).then_inc(S.ldu, 16)
+    g.scalar.dma_start(out=T.Bb[:, :], in_=T.b[:, :]).then_inc(S.ldb, 16)
+
+    cnt = [0]
+
+    def fill(ap, c):
+        V.memset(ap, c).then_inc(S.v, 1)
+        cnt[0] += 1
+
+    def tt(out, a, b, op):
+        V.wait_ge(S.v, cnt[0])
+        V.tensor_tensor(out, a, b, op).then_inc(S.v, 1)
+        cnt[0] += 1
+
+    def cp(out, a):
+        V.wait_ge(S.v, cnt[0])
+        V.tensor_copy(out, a).then_inc(S.v, 1)
+        cnt[0] += 1
+
+    C8, C05, CSC = T.PC[:, 0:64], T.PC[:, 64:128], T.PC[:, 192:194]
+    X, R, R4, ND, NE = T.PW[:, 0:64], T.PW[:, 64:132], T.PW[:, 136:204], T.PW[:, 208:268], T.PW[:, 272:288]
+    fill(C8, 0.125)
+    fill(T.U8[:, 0:4], 0.0)
+    fill(T.U8[:, 68:72], 0.0)
+    fill(C05, 0.5)
+    fill(T.PW[:, 64:66], 0.0)
+    fill(T.PW[:, 130:132], 0.0)
+    fill(T.PC[:, 128:192], -1.0)
+    fill(T.AB[:, 60:64], 0.0)
+    fill(T.NQ[:, 60:64], 0.0)
+    fill(T.SB[:, 0:20], 0.0)
+    fill(T.PC[:, 192:193], -1.0 / 512.0)
+    fill(T.PC[:, 193:194], 1.0)
+
+    V.wait_ge(S.ldu, 16)
+    tt(T.U8[:, 4:68], T.U[:, :], C8, MUL)
+    tt(T.A[:, 0:71], T.U8[:, 0:71], T.U8[:, 1:72], ADD)
+    V.wait_ge(S.ldb, 16)
+    tt(X, T.Bb[:, :], C05, MUL)
+    tt(T.PW[:, 66:130], X, T.U[:, :], SUB)
+    tt(R4, R, T.A[:, 0:68], ADD)
+    tt(T.Dx[:, :], R4, T.A[:, 3:71], ADD)
+    n_dx = cnt[0]
+    tt(ND, T.Dx[:, 4:64], T.PC[:, 128:188], MUL)
+    tt(T.AB[:, 0:60], T.Dx[:, 4:64], ND, MAX)
+    tt(T.NQ[:, 0:60], T.Dx[:, 4:64], ND, MUL)
+    tt(T.TS[:, 0:32], T.NQ[:, 0:32], T.NQ[:, 32:64], ADD)
+    tt(T.TM[:, 0:32], T.AB[:, 0:32], T.AB[:, 32:64], MAX)
+    o, w = 0, 32
+    while w > 2:
+        hw = w // 2
+        tt(T.TS[:, o + w:o + w + hw], T.TS[:, o:o + hw], T.TS[:, o + hw:o + w], ADD)
+        tt(T.TM[:, o + w:o + w + hw], T.TM[:, o:o + hw], T.TM[:, o + hw:o + w], MAX)
+        o, w = o + w, hw
+    tt(T.SB[:, 16:17], T.TS[:, o:o + 1], T.TS[:, o + 1:o + 2], ADD)
+    tt(T.SB[:, 17:18], T.TM[:, o:o + 1], T.TM[:, o + 1:o + 2], MAX)
+    n_pi = cnt[0]
+    cp(T.GR[:, 4 * p:4 * p + 4], T.Dx[:, 64:68])
+    cp(T.GL[:, 4 * (p - 1):4 * p], T.Dx[:, 0:4])
+    cp(T.OT[:, 3:4], T.SB[:, 16:17])
+    cp(T.OT[:, 11:12], T.SB[:, 17:18])
+    pk_total = 0
+    for q in win:
+        if q != x:
+            k = win.index(q)
+            pk_total += ((1 if k < 4 else 0) + (1 if k > 0 else 0)) * (npk if on_chip(q, x) else nlow)
+    V.wait_ge(S.pk, pk_total)
+    tt(T.E[:, :], T.GR[:, :], T.GL[:, :], ADD)
+    tt(NE, T.E[:, :], T.PC[:, 128:144], MUL)
+    tt(T.QE[:, :], T.E[:, :], NE, MUL)
+    tt(T.AE[:, :], T.E[:, :], NE, MAX)
+    tt(T.Q8[:, :], T.QE[:, 0:16:2], T.QE[:, 1:16:2], ADD)
+    tt(T.A8[:, :], T.AE[:, 0:16:2], T.AE[:, 1:16:2], MAX)
+    tt(T.SB[:, 0:16:4], T.Q8[:, 0:8:2], T.Q8[:, 1:8:2], ADD)
+    tt(T.SB[:, 1:16:4], T.A8[:, 0:8:2], T.A8[:, 1:8:2], MAX)
+    n_sb = cnt[0]
+    tt(T.Y[:, 2:62], T.Dx[:, 4:64], T.U[:, 2:62], ADD)
+    tt(T.Y[:, 0:2], T.E[:, 4 * p - 2:4 * p], T.U[:, 0:2], ADD)
+    tt(T.Y[:, 62:64], T.E[:, 4 * p:4 * p + 2], T.U[:, 62:64], ADD)
+    n_y = cnt[0]
+    pi_total = sum(len(high) if on_chip(q, x) else nlow for q in run if q != x)
+    a = 4 * (1 if ix == 0 else 0)
+    V.wait_ge(S.pi, pi_total)
+    tt(T.OT[:, 0:3], T.SB[:, a:a + 12:4], T.SB[:, 20:32:4], ADD)
+    tt(T.OT[:, 8:11], T.SB[:, a + 1:a + 13:4], T.SB[:, 21:32:4], MAX)
+    tt(T.OT[:, 4:6], T.OT[:, 0:2], T.OT[:, 2:4], ADD)
+    tt(T.OT[:, 12:14], T.OT[:, 8:10], T.OT[:, 10:12], MAX)
+    tt(T.RKO[:, 32:33], T.OT[:, 4:5], T.OT[:, 5:6], ADD)
+    tt(T.RKO[:, 33:34], T.OT[:, 12:13], T.OT[:, 13:14], MAX)
+    V.wait_ge(S.fin, 2 * nlow)
+    st = 4 * (8 - jx)
+    tt(T.FT[:, 0:4], T.CA[:, 0:16:4], T.CA[:, 16:32:4], ADD)
+    tt(T.FT[:, 16:20], T.CA[:, 1:16:4], T.CA[:, 17:32:4], MAX)
+    tt(T.FT[:, 4:6], T.FT[:, 0:2], T.FT[:, 2:4], ADD)
+    tt(T.FT[:, 20:22], T.FT[:, 16:18], T.FT[:, 18:20], MAX)
+    tt(T.FT[:, 8:10], T.FT[:, 4:6], T.RKO[:, 4 * jx:33:st], ADD)
+    tt(T.FT[:, 24:26], T.FT[:, 20:22], T.RKO[:, 4 * jx + 1:34:st], MAX)
+    tt(T.SS[:, 0:1], T.FT[:, 8:9], T.FT[:, 9:10], ADD)
+    tt(T.SS[:, 1:2], T.FT[:, 24:25], T.FT[:, 25:26], MAX)
+    tt(T.SO[:, 0:2], T.SS[:, 0:2], CSC, MUL)
+    n_s = cnt[0]
+
+    def xfer(src, dsts, mask, sem):
+        return RemoteDMATransfer(dst_ids=[dst_id(r) for r, _ in dsts], dma_engine_mask=mask, remote_sem=sem,
+                                 srcs=[src], dsts=[ap for _, ap in dsts], alu_op=0)
+
+    needR, needL = [], []
+    for r in range(n):
+        if r == x:
+            continue
+        wr = window(r)[0]
+        if x in wr:
+            k = wr.index(x)
+            if k < 4:
+                needR.append((r, T.GR[:, 4 * k:4 * k + 4]))
+            if k > 0:
+                needL.append((r, T.GL[:, 4 * (k - 1):4 * k]))
+    g.wait_ge(S.v, n_dx)
+    g.remote_dma_fused([
+        xfer(T.Dx[:, 64:68], [d for d in needR if d[0] != peer], lowA, S.pk),
+        xfer(T.Dx[:, 0:4], [d for d in needL if d[0] != peer], lowB, S.pk),
+        xfer(T.Dx[:, 64:68], [d for d in needR if d[0] == peer], sum(high[:npk]), S.pk),
+        xfer(T.Dx[:, 0:4], [d for d in needL if d[0] == peer], sum(high[npk:]), S.pk),
+    ], local_sem=S.sent)
+    sent = 2 * nlow + 2 * npk
+    g.wait_ge(S.v, n_pi)
+    tr, masks = [], [lowA, lowB]
+    for r in run:
+        if r == x:
+            continue
+        slot = 20 + 4 * [m for m in run if m != r].index(x)
+        tr.append(xfer(T.SB[:, 16:20], [(r, T.SB[:, slot:slot + 4])], sum(high) if r == peer else masks.pop(0), S.pi))
+    g.remote_dma_fused(tr, local_sem=S.sent)
+    sent += 2 * nlow + len(high)
+    g.wait_ge(S.v, n_sb)
+    g.wait_ge(S.pi, pi_total)
+    g.remote_dma_fused([
+        xfer(T.SB[:, :], [(cable, T.CA[:, :])], lowA, S.fin),
+        xfer(T.SB[:, :], [(rackp, T.RKO[:, 0:32])], lowB, S.fin),
+    ], local_sem=S.sent)
+    sent += 2 * nlow
+
+    g.scalar.wait_ge(S.v, n_y)
+    g.scalar.dma_start(out=T.y[:, :], in_=T.Y[:, :]).then_inc(S.st, 16)
+    g.sync.wait_ge(S.v, n_s)
+    g.sync.dma_start(out=T.s[:, :], in_=T.SO[:, 0:2]).then_inc(S.st, 16)
+    g.wait_ge(S.sent, sent)
+    g.wait_ge(S.st, 32)

@@ -13,7 +13,7 @@ SCRATCH = {
     "SS": ("sbuf", [128, 4], F), "SO": ("sbuf", [128, 4], F),
     "PC": ("psum", [128, 256], F), "PW": ("psum", [128, 512], F),
 }
-SEMAPHORES = ["ldu", "ldb", "v", "pk", "pi", "fin", "sent", "st"]
+SEMAPHORES = ["ldu", "ldb", "va", "vb", "pk", "pi", "fin", "sent", "st"]
 
 
 def _bits(m):
@@ -72,21 +72,31 @@ def rank_program(g, core, T, topo):
     g.sync.dma_start(out=T.U[:, :], in_=T.u[:, :]).then_inc(S.ldu, 16)
     g.scalar.dma_start(out=T.Bb[:, :], in_=T.b[:, :]).then_inc(S.ldb, 16)
 
-    cnt = [0]
+    sems = [S.va, S.vb]
+    cnt = [0, 0]
 
     def fill(ap, c):
-        V.memset(ap, c).then_inc(S.v, 1)
+        V.memset(ap, c).then_inc(S.va, 1)
         cnt[0] += 1
 
-    def tt(out, a, b, op):
-        V.wait_ge(S.v, cnt[0])
-        V.tensor_tensor(out, a, b, op).then_inc(S.v, 1)
-        cnt[0] += 1
+    def pre(c, join):
+        V.wait_ge(sems[c], cnt[c])
+        if join:
+            V.wait_ge(sems[1 - c], cnt[1 - c])
 
-    def cp(out, a):
-        V.wait_ge(S.v, cnt[0])
-        V.tensor_copy(out, a).then_inc(S.v, 1)
-        cnt[0] += 1
+    def tt(c, out, a, b, op, join=False):
+        pre(c, join)
+        V.tensor_tensor(out, a, b, op).then_inc(sems[c], 1)
+        cnt[c] += 1
+
+    def cp(c, out, a, join=False):
+        pre(c, join)
+        V.tensor_copy(out, a).then_inc(sems[c], 1)
+        cnt[c] += 1
+
+    def both(q, mark):
+        q.wait_ge(S.va, mark[0])
+        q.wait_ge(S.vb, mark[1])
 
     C8, C05, CSC = T.PC[:, 0:64], T.PC[:, 64:128], T.PC[:, 192:194]
     X, R, R4, ND, NE = T.PW[:, 0:64], T.PW[:, 64:132], T.PW[:, 136:204], T.PW[:, 208:268], T.PW[:, 272:288]
@@ -104,72 +114,72 @@ def rank_program(g, core, T, topo):
     fill(T.PC[:, 193:194], 1.0)
 
     V.wait_ge(S.ldu, 16)
-    tt(T.U8[:, 4:68], T.U[:, :], C8, MUL)
-    tt(T.A[:, 0:71], T.U8[:, 0:71], T.U8[:, 1:72], ADD)
+    tt(0, T.U8[:, 4:68], T.U[:, :], C8, MUL)
     V.wait_ge(S.ldb, 16)
-    tt(X, T.Bb[:, :], C05, MUL)
-    tt(T.PW[:, 66:130], X, T.U[:, :], SUB)
-    tt(R4, R, T.A[:, 0:68], ADD)
-    tt(T.Dx[:, :], R4, T.A[:, 3:71], ADD)
-    n_dx = cnt[0]
-    tt(ND, T.Dx[:, 4:64], T.PC[:, 128:188], MUL)
-    tt(T.AB[:, 0:60], T.Dx[:, 4:64], ND, MAX)
-    tt(T.NQ[:, 0:60], T.Dx[:, 4:64], ND, MUL)
-    tt(T.TS[:, 0:32], T.NQ[:, 0:32], T.NQ[:, 32:64], ADD)
-    tt(T.TM[:, 0:32], T.AB[:, 0:32], T.AB[:, 32:64], MAX)
+    tt(1, X, T.Bb[:, :], C05, MUL, join=True)
+    tt(0, T.A[:, 0:71], T.U8[:, 0:71], T.U8[:, 1:72], ADD)
+    tt(1, T.PW[:, 66:130], X, T.U[:, :], SUB)
+    tt(0, R4, R, T.A[:, 0:68], ADD, join=True)
+    tt(0, T.Dx[:, :], R4, T.A[:, 3:71], ADD)
+    n_dx = list(cnt)
+    tt(0, ND, T.Dx[:, 4:64], T.PC[:, 128:188], MUL)
+    tt(0, T.NQ[:, 0:60], T.Dx[:, 4:64], ND, MUL)
+    tt(1, T.AB[:, 0:60], T.Dx[:, 4:64], ND, MAX, join=True)
+    tt(0, T.TS[:, 0:32], T.NQ[:, 0:32], T.NQ[:, 32:64], ADD)
+    tt(1, T.TM[:, 0:32], T.AB[:, 0:32], T.AB[:, 32:64], MAX)
     o, w = 0, 32
     while w > 2:
         hw = w // 2
-        tt(T.TS[:, o + w:o + w + hw], T.TS[:, o:o + hw], T.TS[:, o + hw:o + w], ADD)
-        tt(T.TM[:, o + w:o + w + hw], T.TM[:, o:o + hw], T.TM[:, o + hw:o + w], MAX)
+        tt(0, T.TS[:, o + w:o + w + hw], T.TS[:, o:o + hw], T.TS[:, o + hw:o + w], ADD)
+        tt(1, T.TM[:, o + w:o + w + hw], T.TM[:, o:o + hw], T.TM[:, o + hw:o + w], MAX)
         o, w = o + w, hw
-    tt(T.SB[:, 16:17], T.TS[:, o:o + 1], T.TS[:, o + 1:o + 2], ADD)
-    tt(T.SB[:, 17:18], T.TM[:, o:o + 1], T.TM[:, o + 1:o + 2], MAX)
-    n_pi = cnt[0]
-    cp(T.GR[:, 4 * p:4 * p + 4], T.Dx[:, 64:68])
-    cp(T.GL[:, 4 * (p - 1):4 * p], T.Dx[:, 0:4])
-    cp(T.OT[:, 3:4], T.SB[:, 16:17])
-    cp(T.OT[:, 11:12], T.SB[:, 17:18])
+    tt(0, T.SB[:, 16:17], T.TS[:, o:o + 1], T.TS[:, o + 1:o + 2], ADD)
+    tt(1, T.SB[:, 17:18], T.TM[:, o:o + 1], T.TM[:, o + 1:o + 2], MAX)
+    n_pi = list(cnt)
+    cp(0, T.GR[:, 4 * p:4 * p + 4], T.Dx[:, 64:68])
+    cp(1, T.GL[:, 4 * (p - 1):4 * p], T.Dx[:, 0:4])
+    cp(0, T.OT[:, 3:4], T.SB[:, 16:17])
+    cp(1, T.OT[:, 11:12], T.SB[:, 17:18])
     pk_total = 0
     for q in win:
         if q != x:
             k = win.index(q)
             pk_total += ((1 if k < 4 else 0) + (1 if k > 0 else 0)) * (npk if on_chip(q, x) else nlow)
     V.wait_ge(S.pk, pk_total)
-    tt(T.E[:, :], T.GR[:, :], T.GL[:, :], ADD)
-    tt(NE, T.E[:, :], T.PC[:, 128:144], MUL)
-    tt(T.QE[:, :], T.E[:, :], NE, MUL)
-    tt(T.AE[:, :], T.E[:, :], NE, MAX)
-    tt(T.Q8[:, :], T.QE[:, 0:16:2], T.QE[:, 1:16:2], ADD)
-    tt(T.A8[:, :], T.AE[:, 0:16:2], T.AE[:, 1:16:2], MAX)
-    tt(T.SB[:, 0:16:4], T.Q8[:, 0:8:2], T.Q8[:, 1:8:2], ADD)
-    tt(T.SB[:, 1:16:4], T.A8[:, 0:8:2], T.A8[:, 1:8:2], MAX)
-    n_sb = cnt[0]
-    tt(T.Y[:, 2:62], T.Dx[:, 4:64], T.U[:, 2:62], ADD)
-    tt(T.Y[:, 0:2], T.E[:, 4 * p - 2:4 * p], T.U[:, 0:2], ADD)
-    tt(T.Y[:, 62:64], T.E[:, 4 * p:4 * p + 2], T.U[:, 62:64], ADD)
-    n_y = cnt[0]
+    tt(0, T.E[:, :], T.GR[:, :], T.GL[:, :], ADD, join=True)
+    tt(0, NE, T.E[:, :], T.PC[:, 128:144], MUL)
+    tt(0, T.QE[:, :], T.E[:, :], NE, MUL)
+    tt(1, T.AE[:, :], T.E[:, :], NE, MAX, join=True)
+    tt(0, T.Q8[:, :], T.QE[:, 0:16:2], T.QE[:, 1:16:2], ADD)
+    tt(1, T.A8[:, :], T.AE[:, 0:16:2], T.AE[:, 1:16:2], MAX)
+    tt(0, T.SB[:, 0:16:4], T.Q8[:, 0:8:2], T.Q8[:, 1:8:2], ADD)
+    tt(1, T.SB[:, 1:16:4], T.A8[:, 0:8:2], T.A8[:, 1:8:2], MAX)
+    n_sb = list(cnt)
+    tt(0, T.Y[:, 2:62], T.Dx[:, 4:64], T.U[:, 2:62], ADD)
+    tt(1, T.Y[:, 0:2], T.E[:, 4 * p - 2:4 * p], T.U[:, 0:2], ADD)
+    tt(0, T.Y[:, 62:64], T.E[:, 4 * p:4 * p + 2], T.U[:, 62:64], ADD)
+    n_y = list(cnt)
     pi_total = sum(len(high) if on_chip(q, x) else nlow for q in run if q != x)
     a = 4 * (1 if ix == 0 else 0)
     V.wait_ge(S.pi, pi_total)
-    tt(T.OT[:, 0:3], T.SB[:, a:a + 12:4], T.SB[:, 20:32:4], ADD)
-    tt(T.OT[:, 8:11], T.SB[:, a + 1:a + 13:4], T.SB[:, 21:32:4], MAX)
-    tt(T.OT[:, 4:6], T.OT[:, 0:2], T.OT[:, 2:4], ADD)
-    tt(T.OT[:, 12:14], T.OT[:, 8:10], T.OT[:, 10:12], MAX)
-    tt(T.RKO[:, 32:33], T.OT[:, 4:5], T.OT[:, 5:6], ADD)
-    tt(T.RKO[:, 33:34], T.OT[:, 12:13], T.OT[:, 13:14], MAX)
+    tt(0, T.OT[:, 0:3], T.SB[:, a:a + 12:4], T.SB[:, 20:32:4], ADD)
+    tt(1, T.OT[:, 8:11], T.SB[:, a + 1:a + 13:4], T.SB[:, 21:32:4], MAX)
+    tt(0, T.OT[:, 4:6], T.OT[:, 0:2], T.OT[:, 2:4], ADD)
+    tt(1, T.OT[:, 12:14], T.OT[:, 8:10], T.OT[:, 10:12], MAX)
+    tt(0, T.RKO[:, 32:33], T.OT[:, 4:5], T.OT[:, 5:6], ADD)
+    tt(1, T.RKO[:, 33:34], T.OT[:, 12:13], T.OT[:, 13:14], MAX)
     V.wait_ge(S.fin, 2 * nlow)
     st = 4 * (8 - jx)
-    tt(T.FT[:, 0:4], T.CA[:, 0:16:4], T.CA[:, 16:32:4], ADD)
-    tt(T.FT[:, 16:20], T.CA[:, 1:16:4], T.CA[:, 17:32:4], MAX)
-    tt(T.FT[:, 4:6], T.FT[:, 0:2], T.FT[:, 2:4], ADD)
-    tt(T.FT[:, 20:22], T.FT[:, 16:18], T.FT[:, 18:20], MAX)
-    tt(T.FT[:, 8:10], T.FT[:, 4:6], T.RKO[:, 4 * jx:33:st], ADD)
-    tt(T.FT[:, 24:26], T.FT[:, 20:22], T.RKO[:, 4 * jx + 1:34:st], MAX)
-    tt(T.SS[:, 0:1], T.FT[:, 8:9], T.FT[:, 9:10], ADD)
-    tt(T.SS[:, 1:2], T.FT[:, 24:25], T.FT[:, 25:26], MAX)
-    tt(T.SO[:, 0:2], T.SS[:, 0:2], CSC, MUL)
-    n_s = cnt[0]
+    tt(0, T.FT[:, 0:4], T.CA[:, 0:16:4], T.CA[:, 16:32:4], ADD)
+    tt(1, T.FT[:, 16:20], T.CA[:, 1:16:4], T.CA[:, 17:32:4], MAX)
+    tt(0, T.FT[:, 4:6], T.FT[:, 0:2], T.FT[:, 2:4], ADD)
+    tt(1, T.FT[:, 20:22], T.FT[:, 16:18], T.FT[:, 18:20], MAX)
+    tt(0, T.FT[:, 8:10], T.FT[:, 4:6], T.RKO[:, 4 * jx:33:st], ADD)
+    tt(1, T.FT[:, 24:26], T.FT[:, 20:22], T.RKO[:, 4 * jx + 1:34:st], MAX)
+    tt(0, T.SS[:, 0:1], T.FT[:, 8:9], T.FT[:, 9:10], ADD)
+    tt(1, T.SS[:, 1:2], T.FT[:, 24:25], T.FT[:, 25:26], MAX)
+    tt(0, T.SO[:, 0:2], T.SS[:, 0:2], CSC, MUL, join=True)
+    n_s = list(cnt)
 
     def xfer(src, dsts, mask, sem):
         return RemoteDMATransfer(dst_ids=[dst_id(r) for r, _ in dsts], dma_engine_mask=mask, remote_sem=sem,
@@ -186,7 +196,7 @@ def rank_program(g, core, T, topo):
                 needR.append((r, T.GR[:, 4 * k:4 * k + 4]))
             if k > 0:
                 needL.append((r, T.GL[:, 4 * (k - 1):4 * k]))
-    g.wait_ge(S.v, n_dx)
+    g.wait_ge(S.va, n_dx[0])
     g.remote_dma_fused([
         xfer(T.Dx[:, 64:68], [d for d in needR if d[0] != peer], lowA, S.pk),
         xfer(T.Dx[:, 0:4], [d for d in needL if d[0] != peer], lowB, S.pk),
@@ -194,7 +204,7 @@ def rank_program(g, core, T, topo):
         xfer(T.Dx[:, 0:4], [d for d in needL if d[0] == peer], sum(high[npk:]), S.pk),
     ], local_sem=S.sent)
     sent = 2 * nlow + 2 * npk
-    g.wait_ge(S.v, n_pi)
+    both(g, n_pi)
     tr, masks = [], [lowA, lowB]
     for r in run:
         if r == x:
@@ -203,7 +213,7 @@ def rank_program(g, core, T, topo):
         tr.append(xfer(T.SB[:, 16:20], [(r, T.SB[:, slot:slot + 4])], sum(high) if r == peer else masks.pop(0), S.pi))
     g.remote_dma_fused(tr, local_sem=S.sent)
     sent += 2 * nlow + len(high)
-    g.wait_ge(S.v, n_sb)
+    both(g, n_sb)
     g.wait_ge(S.pi, pi_total)
     g.remote_dma_fused([
         xfer(T.SB[:, :], [(cable, T.CA[:, :])], lowA, S.fin),
@@ -211,9 +221,9 @@ def rank_program(g, core, T, topo):
     ], local_sem=S.sent)
     sent += 2 * nlow
 
-    g.scalar.wait_ge(S.v, n_y)
+    both(g.scalar, n_y)
     g.scalar.dma_start(out=T.y[:, :], in_=T.Y[:, :]).then_inc(S.st, 16)
-    g.sync.wait_ge(S.v, n_s)
+    g.sync.wait_ge(S.va, n_s[0])
     g.sync.dma_start(out=T.s[:, :], in_=T.SO[:, 0:2]).then_inc(S.st, 16)
     g.wait_ge(S.sent, sent)
     g.wait_ge(S.st, 32)

@@ -3,17 +3,18 @@ from concourse.mybir import AluOpType
 
 F = "float32"
 SCRATCH = {
-    "U": ("sbuf", [128, 64], F), "Bb": ("sbuf", [128, 64], F),
-    "U8": ("sbuf", [128, 72], F), "A": ("sbuf", [128, 72], F), "Dx": ("sbuf", [128, 68], F),
+    "Up": ("sbuf", [128, 72], F), "Bb": ("sbuf", [128, 64], F), "U8": ("sbuf", [128, 64], F),
+    "A": ("sbuf", [128, 72], F), "Tt": ("sbuf", [128, 68], F), "DD": ("sbuf", [128, 136], F),
     "AB": ("sbuf", [128, 64], F), "NQ": ("sbuf", [128, 64], F), "TS": ("sbuf", [128, 64], F), "TM": ("sbuf", [128, 64], F),
-    "GR": ("sbuf", [128, 16], F), "GL": ("sbuf", [128, 16], F), "E": ("sbuf", [128, 16], F),
-    "AE": ("sbuf", [128, 16], F), "QE": ("sbuf", [128, 16], F), "Q8": ("sbuf", [128, 8], F), "A8": ("sbuf", [128, 8], F),
-    "SB": ("sbuf", [128, 32], F), "CA": ("sbuf", [128, 32], F), "RKO": ("sbuf", [128, 36], F),
-    "Y": ("sbuf", [128, 64], F), "OT": ("sbuf", [128, 16], F), "FT": ("sbuf", [128, 32], F),
+    "GR": ("sbuf", [128, 32], F), "GL": ("sbuf", [128, 32], F), "EE": ("sbuf", [128, 32], F),
+    "AE": ("sbuf", [128, 16], F), "QE": ("sbuf", [128, 16], F),
+    "SB": ("sbuf", [128, 32], F), "CA": ("sbuf", [128, 32], F), "RK": ("sbuf", [128, 32], F),
+    "Y8": ("sbuf", [128, 64], F), "Y": ("sbuf", [128, 64], F),
+    "OS": ("sbuf", [128, 12], F), "OM": ("sbuf", [128, 12], F), "FS": ("sbuf", [128, 16], F), "FM": ("sbuf", [128, 16], F),
     "SS": ("sbuf", [128, 4], F), "SO": ("sbuf", [128, 4], F),
     "PC": ("psum", [128, 256], F), "PW": ("psum", [128, 512], F),
 }
-SEMAPHORES = ["ldu", "ldb", "va", "vb", "pk", "pi", "fin", "sent", "st"]
+SEMAPHORES = ["ldu", "ldb", "va", "vb", "vc", "pk", "pi", "fin", "sent", "st"]
 
 
 def _bits(m):
@@ -69,62 +70,64 @@ def rank_program(g, core, T, topo):
     lowA, lowB = sum(low[:h]), sum(low[h:])
     nlow, npk = h, len(high) // 2
 
-    g.sync.dma_start(out=T.U[:, :], in_=T.u[:, :]).then_inc(S.ldu, 16)
+    g.sync.dma_start(out=T.Up[:, 4:68], in_=T.u[:, :]).then_inc(S.ldu, 16)
     g.scalar.dma_start(out=T.Bb[:, :], in_=T.b[:, :]).then_inc(S.ldb, 16)
 
-    sems = [S.va, S.vb]
-    cnt = [0, 0]
+    sems = [S.va, S.vb, S.vc]
+    cnt = [0, 0, 0]
 
     def fill(ap, c):
         V.memset(ap, c).then_inc(S.va, 1)
         cnt[0] += 1
 
-    def pre(c, join):
-        V.wait_ge(sems[c], cnt[c])
-        if join:
-            V.wait_ge(sems[1 - c], cnt[1 - c])
-
-    def tt(c, out, a, b, op, join=False):
-        pre(c, join)
+    def tt(c, out, a, b, op, waits=None):
+        for k in ([c] if waits is None else waits):
+            V.wait_ge(sems[k], cnt[k])
         V.tensor_tensor(out, a, b, op).then_inc(sems[c], 1)
         cnt[c] += 1
 
-    def cp(c, out, a, join=False):
-        pre(c, join)
+    def cp(c, out, a, waits=None):
+        for k in ([c] if waits is None else waits):
+            V.wait_ge(sems[k], cnt[k])
         V.tensor_copy(out, a).then_inc(sems[c], 1)
         cnt[c] += 1
 
-    def both(q, mark):
-        q.wait_ge(S.va, mark[0])
-        q.wait_ge(S.vb, mark[1])
+    def after(q, mark, chains):
+        for k in chains:
+            q.wait_ge(sems[k], mark[k])
 
-    C8, C05, CSC = T.PC[:, 0:64], T.PC[:, 64:128], T.PC[:, 192:194]
-    X, R, R4, ND, NE = T.PW[:, 0:64], T.PW[:, 64:132], T.PW[:, 136:204], T.PW[:, 208:268], T.PW[:, 272:288]
-    fill(C8, 0.125)
-    fill(T.U8[:, 0:4], 0.0)
-    fill(T.U8[:, 68:72], 0.0)
-    fill(C05, 0.5)
-    fill(T.PW[:, 64:66], 0.0)
-    fill(T.PW[:, 130:132], 0.0)
-    fill(T.PC[:, 128:192], -1.0)
-    fill(T.AB[:, 60:64], 0.0)
+    C4, C8, C18, CSC = T.PC[:, 0:64], T.PC[:, 64:128], T.PC[:, 128:188], T.PC[:, 192:194]
+    X4, R, NR = T.PW[:, 0:64], T.PW[:, 128:196], T.PW[:, 200:268]
+    fill(T.Up[:, 0:4], 0.0)
+    fill(T.Up[:, 68:72], 0.0)
+    fill(C8, 8.0)
+    fill(C4, 4.0)
+    fill(T.PW[:, 128:130], 0.0)
+    fill(T.PW[:, 194:196], 0.0)
+    fill(T.PW[:, 200:202], 0.0)
+    fill(T.PW[:, 266:268], 0.0)
     fill(T.NQ[:, 60:64], 0.0)
+    fill(T.AB[:, 60:64], 0.0)
     fill(T.SB[:, 0:20], 0.0)
-    fill(T.PC[:, 192:193], -1.0 / 512.0)
-    fill(T.PC[:, 193:194], 1.0)
+    fill(T.OS[:, 3:4], 0.0)
+    fill(T.OM[:, 3:4], 0.0)
+    fill(T.PC[:, 128:192], 0.125)
+    fill(T.PC[:, 192:193], -1.0 / 32768.0)
+    fill(T.PC[:, 193:194], 0.125)
 
     V.wait_ge(S.ldu, 16)
-    tt(0, T.U8[:, 4:68], T.U[:, :], C8, MUL)
+    tt(0, T.A[:, 0:71], T.Up[:, 0:71], T.Up[:, 1:72], ADD)
+    tt(1, T.U8[:, :], T.Up[:, 4:68], C8, MUL, waits=[])
     V.wait_ge(S.ldb, 16)
-    tt(1, X, T.Bb[:, :], C05, MUL, join=True)
-    tt(0, T.A[:, 0:71], T.U8[:, 0:71], T.U8[:, 1:72], ADD)
-    tt(1, T.PW[:, 66:130], X, T.U[:, :], SUB)
-    tt(0, R4, R, T.A[:, 0:68], ADD, join=True)
-    tt(0, T.Dx[:, :], R4, T.A[:, 3:71], ADD)
+    tt(1, X4, T.Bb[:, :], C4, MUL, waits=[])
+    tt(0, T.Tt[:, :], T.A[:, 0:68], T.A[:, 3:71], ADD)
+    tt(1, T.PW[:, 130:194], X4, T.U8[:, :], SUB)
+    tt(2, T.PW[:, 202:266], T.U8[:, :], X4, SUB, waits=[])
+    tt(0, T.DD[:, 0:136:2], T.Tt[:, :], R, ADD, waits=[0, 1])
+    tt(2, T.DD[:, 1:136:2], NR, T.Tt[:, :], SUB)
     n_dx = list(cnt)
-    tt(0, ND, T.Dx[:, 4:64], T.PC[:, 128:188], MUL)
-    tt(0, T.NQ[:, 0:60], T.Dx[:, 4:64], ND, MUL)
-    tt(1, T.AB[:, 0:60], T.Dx[:, 4:64], ND, MAX, join=True)
+    tt(0, T.NQ[:, 0:60], T.DD[:, 8:128:2], T.DD[:, 9:128:2], MUL, waits=[0, 2])
+    tt(1, T.AB[:, 0:60], T.DD[:, 8:128:2], T.DD[:, 9:128:2], MAX, waits=[])
     tt(0, T.TS[:, 0:32], T.NQ[:, 0:32], T.NQ[:, 32:64], ADD)
     tt(1, T.TM[:, 0:32], T.AB[:, 0:32], T.AB[:, 32:64], MAX)
     o, w = 0, 32
@@ -136,49 +139,54 @@ def rank_program(g, core, T, topo):
     tt(0, T.SB[:, 16:17], T.TS[:, o:o + 1], T.TS[:, o + 1:o + 2], ADD)
     tt(1, T.SB[:, 17:18], T.TM[:, o:o + 1], T.TM[:, o + 1:o + 2], MAX)
     n_pi = list(cnt)
-    cp(0, T.GR[:, 4 * p:4 * p + 4], T.Dx[:, 64:68])
-    cp(1, T.GL[:, 4 * (p - 1):4 * p], T.Dx[:, 0:4])
-    cp(0, T.OT[:, 3:4], T.SB[:, 16:17])
-    cp(1, T.OT[:, 11:12], T.SB[:, 17:18])
+    cp(2, T.GR[:, 8 * p:8 * p + 8], T.DD[:, 128:136], waits=[])
+    cp(2, T.GL[:, 8 * (p - 1):8 * p], T.DD[:, 0:8], waits=[])
+    tt(2, T.Y8[:, 2:62], T.DD[:, 8:128:2], C18, MUL, waits=[])
     pk_total = 0
     for q in win:
         if q != x:
             k = win.index(q)
             pk_total += ((1 if k < 4 else 0) + (1 if k > 0 else 0)) * (npk if on_chip(q, x) else nlow)
     V.wait_ge(S.pk, pk_total)
-    tt(0, T.E[:, :], T.GR[:, :], T.GL[:, :], ADD, join=True)
-    tt(0, NE, T.E[:, :], T.PC[:, 128:144], MUL)
-    tt(0, T.QE[:, :], T.E[:, :], NE, MUL)
-    tt(1, T.AE[:, :], T.E[:, :], NE, MAX, join=True)
-    tt(0, T.Q8[:, :], T.QE[:, 0:16:2], T.QE[:, 1:16:2], ADD)
-    tt(1, T.A8[:, :], T.AE[:, 0:16:2], T.AE[:, 1:16:2], MAX)
-    tt(0, T.SB[:, 0:16:4], T.Q8[:, 0:8:2], T.Q8[:, 1:8:2], ADD)
-    tt(1, T.SB[:, 1:16:4], T.A8[:, 0:8:2], T.A8[:, 1:8:2], MAX)
+    tt(0, T.EE[:, :], T.GR[:, :], T.GL[:, :], ADD, waits=[0, 2])
+    tt(0, T.QE[:, :], T.EE[:, 0:32:2], T.EE[:, 1:32:2], MUL)
+    tt(1, T.AE[:, :], T.EE[:, 0:32:2], T.EE[:, 1:32:2], MAX)
+    tt(0, T.SB[:, 0:16:2], T.QE[:, 0:16:2], T.QE[:, 1:16:2], ADD)
+    tt(1, T.SB[:, 1:16:2], T.AE[:, 0:16:2], T.AE[:, 1:16:2], MAX)
     n_sb = list(cnt)
-    tt(0, T.Y[:, 2:62], T.Dx[:, 4:64], T.U[:, 2:62], ADD)
-    tt(1, T.Y[:, 0:2], T.E[:, 4 * p - 2:4 * p], T.U[:, 0:2], ADD)
-    tt(0, T.Y[:, 62:64], T.E[:, 4 * p:4 * p + 2], T.U[:, 62:64], ADD)
-    n_y = list(cnt)
+    tt(2, T.Y8[:, 0:2], T.EE[:, 8 * p - 4:8 * p:2], T.PC[:, 128:130], MUL, waits=[])
+    tt(2, T.Y8[:, 62:64], T.EE[:, 8 * p:8 * p + 4:2], T.PC[:, 128:130], MUL, waits=[])
     pi_total = sum(len(high) if on_chip(q, x) else nlow for q in run if q != x)
     a = 4 * (1 if ix == 0 else 0)
     V.wait_ge(S.pi, pi_total)
-    tt(0, T.OT[:, 0:3], T.SB[:, a:a + 12:4], T.SB[:, 20:32:4], ADD)
-    tt(1, T.OT[:, 8:11], T.SB[:, a + 1:a + 13:4], T.SB[:, 21:32:4], MAX)
-    tt(0, T.OT[:, 4:6], T.OT[:, 0:2], T.OT[:, 2:4], ADD)
-    tt(1, T.OT[:, 12:14], T.OT[:, 8:10], T.OT[:, 10:12], MAX)
-    tt(0, T.RKO[:, 32:33], T.OT[:, 4:5], T.OT[:, 5:6], ADD)
-    tt(1, T.RKO[:, 33:34], T.OT[:, 12:13], T.OT[:, 13:14], MAX)
+    for c, O, FF, op in ((0, T.OS, T.FS, ADD), (1, T.OM, T.FM, MAX)):
+        tt(c, O[:, 0:3], T.SB[:, a + c:a + 6:2], T.SB[:, a + 6 + c:a + 12:2], op)
+        tt(c, O[:, 4:6], T.SB[:, 16 + c:24:4], T.SB[:, 24 + c:32:4], op, waits=[])
+    tt(2, T.Y[:, :], T.Y8[:, :], T.Up[:, 4:68], ADD)
+    n_y = list(cnt)
+    for c, O, FF, op in ((0, T.OS, T.FS, ADD), (1, T.OM, T.FM, MAX)):
+        tt(c, O[:, 8:10], O[:, 0:2], O[:, 2:4], op)
+        tt(c, O[:, 6:7], O[:, 4:5], O[:, 5:6], op, waits=[])
+    for c, O, FF, op in ((0, T.OS, T.FS, ADD), (1, T.OM, T.FM, MAX)):
+        tt(c, O[:, 10:11], O[:, 8:9], O[:, 9:10], op)
+    for c, O, FF, op in ((0, T.OS, T.FS, ADD), (1, T.OM, T.FM, MAX)):
+        tt(c, FF[:, 7:8], O[:, 10:11], O[:, 6:7], op)
     V.wait_ge(S.fin, 2 * nlow)
-    st = 4 * (8 - jx)
-    tt(0, T.FT[:, 0:4], T.CA[:, 0:16:4], T.CA[:, 16:32:4], ADD)
-    tt(1, T.FT[:, 16:20], T.CA[:, 1:16:4], T.CA[:, 17:32:4], MAX)
-    tt(0, T.FT[:, 4:6], T.FT[:, 0:2], T.FT[:, 2:4], ADD)
-    tt(1, T.FT[:, 20:22], T.FT[:, 16:18], T.FT[:, 18:20], MAX)
-    tt(0, T.FT[:, 8:10], T.FT[:, 4:6], T.RKO[:, 4 * jx:33:st], ADD)
-    tt(1, T.FT[:, 24:26], T.FT[:, 20:22], T.RKO[:, 4 * jx + 1:34:st], MAX)
-    tt(0, T.SS[:, 0:1], T.FT[:, 8:9], T.FT[:, 9:10], ADD)
-    tt(1, T.SS[:, 1:2], T.FT[:, 24:25], T.FT[:, 25:26], MAX)
-    tt(0, T.SO[:, 0:2], T.SS[:, 0:2], CSC, MUL, join=True)
+    j = 4 * jx
+    two = ((0, T.FS, ADD), (1, T.FM, MAX))
+    for c, FF, op in two:
+        tt(c, FF[:, 0:4], T.CA[:, c:8:2], T.CA[:, 8 + c:16:2], op)
+    for c, FF, op in two:
+        tt(c, FF[:, 4:6], T.CA[:, 16 + c:24:4], T.CA[:, 24 + c:32:4], op, waits=[])
+    for c, FF, op in two:
+        tt(c, FF[:, 6:7], T.RK[:, j + c:j + c + 1], T.RK[:, j + 2 + c:j + 3 + c], op, waits=[])
+    for c, FF, op in two:
+        tt(c, FF[:, 8:12], FF[:, 0:4], FF[:, 4:8], op)
+    for c, FF, op in two:
+        tt(c, FF[:, 12:14], FF[:, 8:10], FF[:, 10:12], op)
+    for c, FF, op in two:
+        tt(c, T.SS[:, c:c + 1], FF[:, 12:13], FF[:, 13:14], op)
+    tt(0, T.SO[:, 0:2], T.SS[:, 0:2], CSC, MUL, waits=[0, 1])
     n_s = list(cnt)
 
     def xfer(src, dsts, mask, sem):
@@ -193,18 +201,18 @@ def rank_program(g, core, T, topo):
         if x in wr:
             k = wr.index(x)
             if k < 4:
-                needR.append((r, T.GR[:, 4 * k:4 * k + 4]))
+                needR.append((r, T.GR[:, 8 * k:8 * k + 8]))
             if k > 0:
-                needL.append((r, T.GL[:, 4 * (k - 1):4 * k]))
-    g.wait_ge(S.va, n_dx[0])
+                needL.append((r, T.GL[:, 8 * (k - 1):8 * k]))
+    after(g, n_dx, [0, 2])
     g.remote_dma_fused([
-        xfer(T.Dx[:, 64:68], [d for d in needR if d[0] != peer], lowA, S.pk),
-        xfer(T.Dx[:, 0:4], [d for d in needL if d[0] != peer], lowB, S.pk),
-        xfer(T.Dx[:, 64:68], [d for d in needR if d[0] == peer], sum(high[:npk]), S.pk),
-        xfer(T.Dx[:, 0:4], [d for d in needL if d[0] == peer], sum(high[npk:]), S.pk),
+        xfer(T.DD[:, 128:136], [d for d in needR if d[0] != peer], lowA, S.pk),
+        xfer(T.DD[:, 0:8], [d for d in needL if d[0] != peer], lowB, S.pk),
+        xfer(T.DD[:, 128:136], [d for d in needR if d[0] == peer], sum(high[:npk]), S.pk),
+        xfer(T.DD[:, 0:8], [d for d in needL if d[0] == peer], sum(high[npk:]), S.pk),
     ], local_sem=S.sent)
     sent = 2 * nlow + 2 * npk
-    both(g, n_pi)
+    after(g, n_pi, [0, 1])
     tr, masks = [], [lowA, lowB]
     for r in run:
         if r == x:
@@ -213,17 +221,17 @@ def rank_program(g, core, T, topo):
         tr.append(xfer(T.SB[:, 16:20], [(r, T.SB[:, slot:slot + 4])], sum(high) if r == peer else masks.pop(0), S.pi))
     g.remote_dma_fused(tr, local_sem=S.sent)
     sent += 2 * nlow + len(high)
-    both(g, n_sb)
+    after(g, n_sb, [0, 1])
     g.wait_ge(S.pi, pi_total)
     g.remote_dma_fused([
         xfer(T.SB[:, :], [(cable, T.CA[:, :])], lowA, S.fin),
-        xfer(T.SB[:, :], [(rackp, T.RKO[:, 0:32])], lowB, S.fin),
+        xfer(T.SB[:, :], [(rackp, T.RK[:, :])], lowB, S.fin),
     ], local_sem=S.sent)
     sent += 2 * nlow
 
-    both(g.scalar, n_y)
+    after(g.scalar, n_y, [2])
     g.scalar.dma_start(out=T.y[:, :], in_=T.Y[:, :]).then_inc(S.st, 16)
-    g.sync.wait_ge(S.va, n_s[0])
+    after(g.sync, n_s, [0])
     g.sync.dma_start(out=T.s[:, :], in_=T.SO[:, 0:2]).then_inc(S.st, 16)
     g.wait_ge(S.sent, sent)
     g.wait_ge(S.st, 32)

@@ -1,20 +1,19 @@
 from concourse.bass import DstId, RemoteDMATransfer
-from concourse.mybir import AluOpType
+from concourse.mybir import AluOpType, AxisListType, ActivationFunctionType
 
 F = "float32"
+W = 12
 SCRATCH = {
-    "Up": ("sbuf", [128, 72], F), "Bb": ("sbuf", [128, 64], F), "U8": ("sbuf", [128, 64], F),
-    "A": ("sbuf", [128, 72], F), "Tt": ("sbuf", [128, 68], F), "DD": ("sbuf", [128, 136], F),
-    "AB": ("sbuf", [128, 64], F), "NQ": ("sbuf", [128, 64], F), "TS": ("sbuf", [128, 64], F), "TM": ("sbuf", [128, 64], F),
-    "GR": ("sbuf", [128, 32], F), "GL": ("sbuf", [128, 32], F), "EE": ("sbuf", [128, 32], F),
-    "AE": ("sbuf", [128, 16], F), "QE": ("sbuf", [128, 16], F),
-    "SB": ("sbuf", [128, 32], F), "CA": ("sbuf", [128, 32], F), "RK": ("sbuf", [128, 32], F),
-    "Y8": ("sbuf", [128, 64], F), "Y": ("sbuf", [128, 64], F),
-    "OS": ("sbuf", [128, 12], F), "OM": ("sbuf", [128, 12], F), "FS": ("sbuf", [128, 16], F), "FM": ("sbuf", [128, 16], F),
-    "SS": ("sbuf", [128, 4], F), "SO": ("sbuf", [128, 4], F),
-    "PC": ("psum", [128, 256], F), "PW": ("psum", [128, 512], F),
+    "Up": ("sbuf", [128, 72], F), "Bb": ("sbuf", [128, 64], F), "B4": ("sbuf", [128, 64], F),
+    "A": ("sbuf", [128, 72], F), "Tt": ("sbuf", [128, 68], F), "DY": ("sbuf", [128, 64], F),
+    "Tb": ("sbuf", [128, 9, W], F), "SQ": ("sbuf", [128, 64], F), "SQ2": ("sbuf", [128, 32], F),
+    "Y8": ("sbuf", [128, 64], F), "Y": ("sbuf", [128, 64], F), "YB": ("sbuf", [128, 4], F),
+    "EE": ("sbuf", [128, 32], F), "PP": ("sbuf", [128, 4], F), "CS": ("sbuf", [128, 4], F), "CM": ("sbuf", [128, 4], F),
+    "SO": ("sbuf", [128, 4], F),
+    "PU": ("psum", [128, 512], F), "PR": ("psum", [128, 512], F),
 }
-SEMAPHORES = ["ldu", "ldb", "va", "vb", "vc", "pk", "pi", "fin", "sent", "st"]
+SEMAPHORES = ["ldu", "ldb", "ms", "su", "sA", "sR", "sT", "sD", "sM", "sX", "sQ", "sC", "sY8", "sY", "sYB",
+              "sE", "sP", "sFm", "sFs", "sS", "h1", "fw", "h2", "sent", "st"]
 
 
 def _bits(m):
@@ -25,213 +24,144 @@ def _plan(T, topo):
     cores = list(T.cores)
     n = len(cores)
 
-    def rack(r):
-        return topo.rack(topo.host(cores[r]))
-
-    def window(x):
-        mem = [q for q in range(n) if rack(q) == rack(x)]
-        start = [q for q in mem if (q - 1) % n not in mem][0]
-        run = [(start + i) % n for i in range(len(mem))]
-        prev, nxt = (start - 1) % n, (run[-1] + 1) % n
-        if topo.may_write(cores[prev], cores[x]):
-            return [prev] + run, 0, run
-        return run + [nxt], len(run) - 1, run
-
-    def partner(x, same_rack):
-        return [y for y in range(n) if topo.host(cores[y]) != topo.host(cores[x]) and (rack(y) == rack(x)) == same_rack
-                and topo.may_write(cores[x], cores[y]) and topo.die(cores[y]) == topo.die(cores[x])][0]
-
     def on_chip(a, b):
         return topo.host(cores[a]) == topo.host(cores[b]) and topo.chip(cores[a]) == topo.chip(cores[b])
 
-    return cores, n, window, partner, on_chip
+    def far(y):
+        return [q for q in range(n) if q != y and not topo.may_write(cores[q], cores[y])]
+
+    def relay(y):
+        c = [z for z in range(n) if z != y and not on_chip(z, y) and topo.may_write(cores[z], cores[y])
+             and topo.die(cores[z]) == topo.die(cores[y]) and all(topo.may_write(cores[q], cores[z]) for q in far(y))]
+        return min(c, key=lambda z: (z - y) % n)
+
+    return cores, n, on_chip, far, relay
 
 
 def rank_program(g, core, T, topo):
     x = T.rank_of(core)
     if x is None:
         return
-    cores, n, window, partner, on_chip = _plan(T, topo)
-    S, V = T.sem, g.vector
+    cores, n, on_chip, far, relay = _plan(T, topo)
+    S, V, SC, SY = T.sem, g.vector, g.scalar, g.sync
     ADD, SUB, MUL, MAX = AluOpType.add, AluOpType.subtract, AluOpType.mult, AluOpType.max
-    win, ix, run = window(x)
-    p = win.index(x)
-    cable, rackp = partner(x, False), partner(x, True)
-    jx = window(rackp)[1]
+    AX, ACT = AxisListType.X, ActivationFunctionType
 
     def dst_id(r):
         rid, pid = topo.addr(cores[r], core)
         return DstId(rid=rid, pnc=pid)
 
+    def forwards(z):
+        return [q for y in range(n) if relay(y) == z for q in far(y)]
+
     peer = [r for r in range(n) if r != x and on_chip(r, x)][0]
-    low = _bits(topo.mask(core, cores[cable]))
-    high = [e for e in _bits(topo.mask(core, cores[peer])) if e not in low][:4]
+    direct = [r for r in range(n) if r != x and r != peer and topo.may_write(core, cores[r])]
+    low = _bits(topo.mask(core, cores[direct[0]]))
+    high = [e for e in _bits(topo.mask(core, cores[peer])) if e not in low]
     h = len(low) // 2
-    lowA, lowB = sum(low[:h]), sum(low[h:])
-    nlow, npk = h, len(high) // 2
+    npeer = 2
+    m_fw, m_h1, m_peer, m_all = sum(low[:h]), sum(low[h:]), sum(high[:npeer]), sum(low)
 
-    g.sync.dma_start(out=T.Up[:, 4:68], in_=T.u[:, :]).then_inc(S.ldu, 16)
-    g.scalar.dma_start(out=T.Bb[:, :], in_=T.b[:, :]).then_inc(S.ldb, 16)
+    SY.dma_start(out=T.Up[:, 4:68], in_=T.u[:, :]).then_inc(S.ldu, 16)
+    SC.dma_start(out=T.Bb[:, :], in_=T.b[:, :]).then_inc(S.ldb, 16)
 
-    sems = [S.va, S.vb, S.vc]
-    cnt = [0, 0, 0]
+    U8 = T.PU[:, 0:64]
+    M = T.Tb[:, 0, :]
 
-    def fill(ap, c):
-        V.memset(ap, c).then_inc(S.va, 1)
-        cnt[0] += 1
+    V.memset(T.Up[:, 0:4], 0.0).then_inc(S.ms, 1)
+    V.memset(T.Up[:, 68:72], 0.0).then_inc(S.ms, 1)
+    V.memset(T.PR[:, 0:2], 0.0).then_inc(S.ms, 1)
+    V.memset(T.PR[:, 66:68], 0.0).then_inc(S.ms, 1)
+    V.memset(T.Tb[:, 0, 10:12], 0.0).then_inc(S.ms, 1)
 
-    def tt(c, out, a, b, op, waits=None):
-        for k in ([c] if waits is None else waits):
-            V.wait_ge(sems[k], cnt[k])
-        V.tensor_tensor(out, a, b, op).then_inc(sems[c], 1)
-        cnt[c] += 1
+    SC.wait_ge(S.ldu, 16)
+    SC.activation(U8, T.Up[:, 4:68], ACT.Copy, scale=8.0).then_inc(S.su, 1)
+    SC.wait_ge(S.ldb, 16)
+    SC.activation(T.B4[:, :], T.Bb[:, :], ACT.Copy, scale=4.0).then_inc(S.su, 1)
 
-    def cp(c, out, a, waits=None):
-        for k in ([c] if waits is None else waits):
-            V.wait_ge(sems[k], cnt[k])
-        V.tensor_copy(out, a).then_inc(sems[c], 1)
-        cnt[c] += 1
-
-    def after(q, mark, chains):
-        for k in chains:
-            q.wait_ge(sems[k], mark[k])
-
-    C4, C8, C18, CSC = T.PC[:, 0:64], T.PC[:, 64:128], T.PC[:, 128:188], T.PC[:, 192:194]
-    X4, R, NR = T.PW[:, 0:64], T.PW[:, 128:196], T.PW[:, 200:268]
-    fill(T.Up[:, 0:4], 0.0)
-    fill(T.Up[:, 68:72], 0.0)
-    fill(C8, 8.0)
-    fill(C4, 4.0)
-    fill(T.PW[:, 128:130], 0.0)
-    fill(T.PW[:, 194:196], 0.0)
-    fill(T.PW[:, 200:202], 0.0)
-    fill(T.PW[:, 266:268], 0.0)
-    fill(T.NQ[:, 60:64], 0.0)
-    fill(T.AB[:, 60:64], 0.0)
-    fill(T.SB[:, 0:20], 0.0)
-    fill(T.OS[:, 3:4], 0.0)
-    fill(T.OM[:, 3:4], 0.0)
-    fill(T.PC[:, 128:192], 0.125)
-    fill(T.PC[:, 192:193], -1.0 / 32768.0)
-    fill(T.PC[:, 193:194], 0.125)
-
+    V.wait_ge(S.ms, 5)
     V.wait_ge(S.ldu, 16)
-    tt(0, T.A[:, 0:71], T.Up[:, 0:71], T.Up[:, 1:72], ADD)
-    tt(1, T.U8[:, :], T.Up[:, 4:68], C8, MUL, waits=[])
-    V.wait_ge(S.ldb, 16)
-    tt(1, X4, T.Bb[:, :], C4, MUL, waits=[])
-    tt(0, T.Tt[:, :], T.A[:, 0:68], T.A[:, 3:71], ADD)
-    tt(1, T.PW[:, 130:194], X4, T.U8[:, :], SUB)
-    tt(2, T.PW[:, 202:266], T.U8[:, :], X4, SUB, waits=[])
-    tt(0, T.DD[:, 0:136:2], T.Tt[:, :], R, ADD, waits=[0, 1])
-    tt(2, T.DD[:, 1:136:2], NR, T.Tt[:, :], SUB)
-    n_dx = list(cnt)
-    tt(0, T.NQ[:, 0:60], T.DD[:, 8:128:2], T.DD[:, 9:128:2], MUL, waits=[0, 2])
-    tt(1, T.AB[:, 0:60], T.DD[:, 8:128:2], T.DD[:, 9:128:2], MAX, waits=[])
-    tt(0, T.TS[:, 0:32], T.NQ[:, 0:32], T.NQ[:, 32:64], ADD)
-    tt(1, T.TM[:, 0:32], T.AB[:, 0:32], T.AB[:, 32:64], MAX)
-    o, w = 0, 32
-    while w > 2:
-        hw = w // 2
-        tt(0, T.TS[:, o + w:o + w + hw], T.TS[:, o:o + hw], T.TS[:, o + hw:o + w], ADD)
-        tt(1, T.TM[:, o + w:o + w + hw], T.TM[:, o:o + hw], T.TM[:, o + hw:o + w], MAX)
-        o, w = o + w, hw
-    tt(0, T.SB[:, 16:17], T.TS[:, o:o + 1], T.TS[:, o + 1:o + 2], ADD)
-    tt(1, T.SB[:, 17:18], T.TM[:, o:o + 1], T.TM[:, o + 1:o + 2], MAX)
-    n_pi = list(cnt)
-    cp(2, T.GR[:, 8 * p:8 * p + 8], T.DD[:, 128:136], waits=[])
-    cp(2, T.GL[:, 8 * (p - 1):8 * p], T.DD[:, 0:8], waits=[])
-    tt(2, T.Y8[:, 2:62], T.DD[:, 8:128:2], C18, MUL, waits=[])
-    pk_total = 0
-    for q in win:
-        if q != x:
-            k = win.index(q)
-            pk_total += ((1 if k < 4 else 0) + (1 if k > 0 else 0)) * (npk if on_chip(q, x) else nlow)
-    V.wait_ge(S.pk, pk_total)
-    tt(0, T.EE[:, :], T.GR[:, :], T.GL[:, :], ADD, waits=[0, 2])
-    tt(0, T.QE[:, :], T.EE[:, 0:32:2], T.EE[:, 1:32:2], MUL)
-    tt(1, T.AE[:, :], T.EE[:, 0:32:2], T.EE[:, 1:32:2], MAX)
-    tt(0, T.SB[:, 0:16:2], T.QE[:, 0:16:2], T.QE[:, 1:16:2], ADD)
-    tt(1, T.SB[:, 1:16:2], T.AE[:, 0:16:2], T.AE[:, 1:16:2], MAX)
-    n_sb = list(cnt)
-    tt(2, T.Y8[:, 0:2], T.EE[:, 8 * p - 4:8 * p:2], T.PC[:, 128:130], MUL, waits=[])
-    tt(2, T.Y8[:, 62:64], T.EE[:, 8 * p:8 * p + 4:2], T.PC[:, 128:130], MUL, waits=[])
-    pi_total = sum(len(high) if on_chip(q, x) else nlow for q in run if q != x)
-    a = 4 * (1 if ix == 0 else 0)
-    V.wait_ge(S.pi, pi_total)
-    for c, O, FF, op in ((0, T.OS, T.FS, ADD), (1, T.OM, T.FM, MAX)):
-        tt(c, O[:, 0:3], T.SB[:, a + c:a + 6:2], T.SB[:, a + 6 + c:a + 12:2], op)
-        tt(c, O[:, 4:6], T.SB[:, 16 + c:24:4], T.SB[:, 24 + c:32:4], op, waits=[])
-    tt(2, T.Y[:, :], T.Y8[:, :], T.Up[:, 4:68], ADD)
-    n_y = list(cnt)
-    for c, O, FF, op in ((0, T.OS, T.FS, ADD), (1, T.OM, T.FM, MAX)):
-        tt(c, O[:, 8:10], O[:, 0:2], O[:, 2:4], op)
-        tt(c, O[:, 6:7], O[:, 4:5], O[:, 5:6], op, waits=[])
-    for c, O, FF, op in ((0, T.OS, T.FS, ADD), (1, T.OM, T.FM, MAX)):
-        tt(c, O[:, 10:11], O[:, 8:9], O[:, 9:10], op)
-    for c, O, FF, op in ((0, T.OS, T.FS, ADD), (1, T.OM, T.FM, MAX)):
-        tt(c, FF[:, 7:8], O[:, 10:11], O[:, 6:7], op)
-    V.wait_ge(S.fin, 2 * nlow)
-    j = 4 * jx
-    two = ((0, T.FS, ADD), (1, T.FM, MAX))
-    for c, FF, op in two:
-        tt(c, FF[:, 0:4], T.CA[:, c:8:2], T.CA[:, 8 + c:16:2], op)
-    for c, FF, op in two:
-        tt(c, FF[:, 4:6], T.CA[:, 16 + c:24:4], T.CA[:, 24 + c:32:4], op, waits=[])
-    for c, FF, op in two:
-        tt(c, FF[:, 6:7], T.RK[:, j + c:j + c + 1], T.RK[:, j + 2 + c:j + 3 + c], op, waits=[])
-    for c, FF, op in two:
-        tt(c, FF[:, 8:12], FF[:, 0:4], FF[:, 4:8], op)
-    for c, FF, op in two:
-        tt(c, FF[:, 12:14], FF[:, 8:10], FF[:, 10:12], op)
-    for c, FF, op in two:
-        tt(c, T.SS[:, c:c + 1], FF[:, 12:13], FF[:, 13:14], op)
-    tt(0, T.SO[:, 0:2], T.SS[:, 0:2], CSC, MUL, waits=[0, 1])
-    n_s = list(cnt)
+    V.tensor_tensor(T.A[:, 0:71], T.Up[:, 0:71], T.Up[:, 1:72], ADD).then_inc(S.sA, 1)
+    V.wait_ge(S.su, 2)
+    V.tensor_tensor(T.PR[:, 2:66], T.B4[:, :], U8, SUB).then_inc(S.sR, 1)
+    V.wait_ge(S.sA, 1)
+    V.tensor_tensor(T.Tt[:, :], T.A[:, 0:68], T.A[:, 3:71], ADD).then_inc(S.sT, 1)
+    V.wait_ge(S.sT, 1)
+    V.wait_ge(S.sR, 1)
+    V.tensor_tensor(T.DY[:, :], T.Tt[:, 2:66], T.PR[:, 2:66], ADD).then_inc(S.sD, 1)
+    V.tensor_tensor(T.Tb[:, 0, 0:4], T.Tt[:, 0:4], T.PR[:, 0:4], ADD).then_inc(S.sM, 1)
+    V.tensor_tensor(T.Tb[:, 0, 4:8], T.Tt[:, 64:68], T.PR[:, 64:68], ADD).then_inc(S.sM, 1)
+    V.wait_ge(S.sD, 1)
+    V.tensor_reduce(T.Tb[:, 0, 9:10], T.DY[:, 2:62], AX, MAX, apply_absolute_value=True).then_inc(S.sX, 1)
+    SC.wait_ge(S.sD, 1)
+    SC.activation(T.SQ[:, 0:60], T.DY[:, 2:62], ACT.Square, scale=0.125, accum_out=T.Tb[:, 0, 8:9]).then_inc(S.sQ, 1)
 
     def xfer(src, dsts, mask, sem):
         return RemoteDMATransfer(dst_ids=[dst_id(r) for r, _ in dsts], dma_engine_mask=mask, remote_sem=sem,
                                  srcs=[src], dsts=[ap for _, ap in dsts], alu_op=0)
 
-    needR, needL = [], []
-    for r in range(n):
-        if r == x:
-            continue
-        wr = window(r)[0]
-        if x in wr:
-            k = wr.index(x)
-            if k < 4:
-                needR.append((r, T.GR[:, 8 * k:8 * k + 8]))
-            if k > 0:
-                needL.append((r, T.GL[:, 8 * (k - 1):8 * k]))
-    after(g, n_dx, [0, 2])
-    g.remote_dma_fused([
-        xfer(T.DD[:, 128:136], [d for d in needR if d[0] != peer], lowA, S.pk),
-        xfer(T.DD[:, 0:8], [d for d in needL if d[0] != peer], lowB, S.pk),
-        xfer(T.DD[:, 128:136], [d for d in needR if d[0] == peer], sum(high[:npk]), S.pk),
-        xfer(T.DD[:, 0:8], [d for d in needL if d[0] == peer], sum(high[npk:]), S.pk),
-    ], local_sem=S.sent)
-    sent = 2 * nlow + 2 * npk
-    after(g, n_pi, [0, 1])
-    tr, masks = [], [lowA, lowB]
-    for r in run:
-        if r == x:
-            continue
-        slot = 20 + 4 * [m for m in run if m != r].index(x)
-        tr.append(xfer(T.SB[:, 16:20], [(r, T.SB[:, slot:slot + 4])], sum(high) if r == peer else masks.pop(0), S.pi))
-    g.remote_dma_fused(tr, local_sem=S.sent)
-    sent += 2 * nlow + len(high)
-    after(g, n_sb, [0, 1])
-    g.wait_ge(S.pi, pi_total)
-    g.remote_dma_fused([
-        xfer(T.SB[:, :], [(cable, T.CA[:, :])], lowA, S.fin),
-        xfer(T.SB[:, :], [(rackp, T.RK[:, :])], lowB, S.fin),
-    ], local_sem=S.sent)
-    sent += 2 * nlow
+    def slot(r, q):
+        return (q - r) % n
 
-    after(g.scalar, n_y, [2])
-    g.scalar.dma_start(out=T.y[:, :], in_=T.Y[:, :]).then_inc(S.st, 16)
-    after(g.sync, n_s, [0])
-    g.sync.dma_start(out=T.s[:, :], in_=T.SO[:, 0:2]).then_inc(S.st, 16)
+    to_fw = [r for r in direct if x in forwards(r)]
+    to_h1 = [r for r in direct if x not in forwards(r)]
+    g.wait_ge(S.ms, 5)
+    g.wait_ge(S.sM, 2)
+    g.wait_ge(S.sX, 1)
+    g.wait_ge(S.sQ, 1)
+    g.remote_dma_fused([
+        xfer(M, [(r, T.Tb[:, slot(r, x), :]) for r in to_fw], m_fw, S.fw),
+        xfer(M, [(r, T.Tb[:, slot(r, x), :]) for r in to_h1], m_h1, S.h1),
+        xfer(M, [(peer, T.Tb[:, slot(peer, x), :])], m_peer, S.h1),
+    ], local_sem=S.sent)
+    sent = 2 * h + npeer
+    fw_total = h * len(forwards(x))
+    h1_total = h * len([q for q in direct if q not in forwards(x)]) + npeer
+
+    g.wait_ge(S.fw, fw_total)
+    for y in range(n):
+        if relay(y) == x:
+            k0, j0, m = min(slot(x, q) for q in far(y)), min(slot(y, q) for q in far(y)), len(far(y))
+            g.remote_dma_fused([xfer(T.Tb[:, k0:k0 + m, :], [(y, T.Tb[:, j0:j0 + m, :])], m_all, S.h2)], local_sem=S.sent)
+            sent += 2 * h
+    h2_total = 2 * h
+
+    V.tensor_tensor(T.Tb[:, n, 0:4], T.Tt[:, 0:4], T.PR[:, 0:4], ADD).then_inc(S.sC, 1)
+    V.tensor_scalar(T.Y8[:, :], T.DY[:, :], 0.125, None, MUL).then_inc(S.sY8, 1)
+    V.wait_ge(S.sY8, 1)
+    V.tensor_tensor(T.YB[:, 0:2], T.Y8[:, 0:2], T.Up[:, 4:6], ADD).then_inc(S.sYB, 1)
+    V.tensor_tensor(T.YB[:, 2:4], T.Y8[:, 62:64], T.Up[:, 66:68], ADD).then_inc(S.sYB, 1)
+    V.tensor_tensor(T.Y[:, 2:62], T.Y8[:, 2:62], T.Up[:, 6:66], ADD).then_inc(S.sY, 1)
+    SC.wait_ge(S.sYB, 2)
+    SC.wait_ge(S.h1, h1_total)
+    SC.wait_ge(S.fw, fw_total)
+    for c, src, k in ((0, T.Tb[:, n - 1, 6:7], 0), (1, T.Tb[:, n - 1, 7:8], 1), (62, T.Tb[:, 1, 0:1], 2), (63, T.Tb[:, 1, 1:2], 3)):
+        SC.activation(T.Y[:, c:c + 1], src, ACT.Identity, bias=T.YB[:, k:k + 1], scale=0.125).then_inc(S.sY, 1)
+    SY.wait_ge(S.sY, 5)
+    SY.dma_start(out=T.y[:, :], in_=T.Y[:, :]).then_inc(S.st, 16)
+
+    V.wait_ge(S.sM, 2)
+    V.wait_ge(S.sX, 1)
+    V.wait_ge(S.sQ, 1)
+    V.wait_ge(S.sC, 1)
+    V.wait_ge(S.h1, h1_total)
+    V.wait_ge(S.fw, fw_total)
+    V.wait_ge(S.h2, h2_total)
+    V.tensor_tensor(T.EE[:, :], T.Tb[:, 0:n, 4:8], T.Tb[:, 1:n + 1, 0:4], ADD).then_inc(S.sE, 1)
+    V.tensor_reduce(T.PP[:, 1:2], T.Tb[:, 0:n, 9], AX, MAX).then_inc(S.sP, 1)
+    V.tensor_reduce(T.PP[:, 0:1], T.Tb[:, 0:n, 8], AX, ADD).then_inc(S.sP, 1)
+    V.wait_ge(S.sE, 1)
+    V.tensor_reduce(T.CM[:, 0:1], T.EE[:, :], AX, MAX, apply_absolute_value=True).then_inc(S.sFm, 1)
+    SC.wait_ge(S.sE, 1)
+    SC.activation(T.SQ2[:, :], T.EE[:, :], ACT.Square, scale=0.125, accum_out=T.CS[:, 0:1]).then_inc(S.sFs, 1)
+    V.wait_ge(S.sP, 2)
+    V.wait_ge(S.sFs, 1)
+    V.tensor_scalar(T.SO[:, 0:1], T.CS[:, 0:1], T.PP[:, 0:1], 1.0 / 512.0, ADD, MUL).then_inc(S.sS, 1)
+    V.wait_ge(S.sFm, 1)
+    V.tensor_scalar(T.SO[:, 1:2], T.CM[:, 0:1], T.PP[:, 1:2], 0.125, MAX, MUL).then_inc(S.sS, 1)
+    SY.wait_ge(S.sS, 2)
+    SY.dma_start(out=T.s[:, :], in_=T.SO[:, 0:2]).then_inc(S.st, 16)
     g.wait_ge(S.sent, sent)
+    g.wait_ge(S.h1, h1_total)
+    g.wait_ge(S.h2, h2_total)
     g.wait_ge(S.st, 32)

@@ -7,13 +7,14 @@ SCRATCH = {
     "Up": ("sbuf", [128, 72], F), "Bb": ("sbuf", [128, 64], F), "B4": ("sbuf", [128, 64], F),
     "A": ("sbuf", [128, 72], F), "Tt": ("sbuf", [128, 68], F), "DY": ("sbuf", [128, 64], F),
     "Tb": ("sbuf", [128, 9, W], F), "SQ": ("sbuf", [128, 64], F), "SQ2": ("sbuf", [128, 32], F),
-    "Y8": ("sbuf", [128, 64], F), "Y": ("sbuf", [128, 64], F), "YB": ("sbuf", [128, 4], F),
+    "Y8": ("sbuf", [128, 64], F), "Y": ("sbuf", [128, 64], F), "YB": ("sbuf", [128, 4], F), "YC": ("sbuf", [128, 4], F),
+    "HB": ("sbuf", [128, 4], F),
     "EE": ("sbuf", [128, 32], F), "PP": ("sbuf", [128, 4], F), "CS": ("sbuf", [128, 4], F), "CM": ("sbuf", [128, 4], F),
     "SO": ("sbuf", [128, 4], F),
     "PU": ("psum", [128, 512], F), "PR": ("psum", [128, 512], F),
 }
-SEMAPHORES = ["ldu", "ldb", "ms", "su", "sA", "sR", "sT", "sD", "sM", "sX", "sQ", "sC", "sY8", "sY", "sYB",
-              "sE", "sP", "sFm", "sFs", "sS", "h1", "fw", "h2", "sent", "st"]
+SEMAPHORES = ["ldu", "ldb", "ms", "su", "sA", "sR", "sT", "sD", "sM", "sX", "sQ", "sC", "sY8", "sY", "sYB", "sYC",
+              "sE", "sP", "sFm", "sFs", "sS", "hl", "h1", "fw", "h2", "sent", "st"]
 
 
 def _bits(m):
@@ -54,16 +55,28 @@ def rank_program(g, core, T, topo):
     def forwards(z):
         return [q for y in range(n) if relay(y) == z for q in far(y)]
 
+    def xfer(src, dsts, mask, sem):
+        return RemoteDMATransfer(dst_ids=[dst_id(r) for r, _ in dsts], dma_engine_mask=mask, remote_sem=sem,
+                                 srcs=[src], dsts=[ap for _, ap in dsts], alu_op=0)
+
     peer = [r for r in range(n) if r != x and on_chip(r, x)][0]
     direct = [r for r in range(n) if r != x and r != peer and topo.may_write(core, cores[r])]
     low = _bits(topo.mask(core, cores[direct[0]]))
     high = [e for e in _bits(topo.mask(core, cores[peer])) if e not in low]
-    h = len(low) // 2
-    npeer = 2
-    m_fw, m_h1, m_peer, m_all = sum(low[:h]), sum(low[h:]), sum(high[:npeer]), sum(low)
+    nlow, npeer = len(low), 2
+    m_peer, m_all = sum(high[:npeer]), sum(low)
 
     SY.dma_start(out=T.Up[:, 4:68], in_=T.u[:, :]).then_inc(S.ldu, 16)
     SC.dma_start(out=T.Bb[:, :], in_=T.b[:, :]).then_inc(S.ldb, 16)
+
+    left, right = (x - 1) % n, (x + 1) % n
+    g.wait_ge(S.ldu, 16)
+    g.remote_dma_fused([
+        xfer(T.Up[:, 4:6], [(left, T.HB[:, 2:4])], m_peer if left == peer else m_all, S.hl),
+        xfer(T.Up[:, 66:68], [(right, T.HB[:, 0:2])], m_peer if right == peer else m_all, S.hl),
+    ], local_sem=S.sent)
+    sent = nlow + npeer
+    hl_total = nlow + npeer
 
     U8 = T.PU[:, 0:64]
     M = T.Tb[:, 0, :]
@@ -96,10 +109,6 @@ def rank_program(g, core, T, topo):
     SC.wait_ge(S.sD, 1)
     SC.activation(T.SQ[:, 0:60], T.DY[:, 2:62], ACT.Square, scale=0.125, accum_out=T.Tb[:, 0, 8:9]).then_inc(S.sQ, 1)
 
-    def xfer(src, dsts, mask, sem):
-        return RemoteDMATransfer(dst_ids=[dst_id(r) for r, _ in dsts], dma_engine_mask=mask, remote_sem=sem,
-                                 srcs=[src], dsts=[ap for _, ap in dsts], alu_op=0)
-
     def slot(r, q):
         return (q - r) % n
 
@@ -109,22 +118,22 @@ def rank_program(g, core, T, topo):
     g.wait_ge(S.sM, 2)
     g.wait_ge(S.sX, 1)
     g.wait_ge(S.sQ, 1)
+    g.remote_dma_fused([xfer(M, [(r, T.Tb[:, slot(r, x), :]) for r in to_fw], m_all, S.fw)], local_sem=S.sent)
     g.remote_dma_fused([
-        xfer(M, [(r, T.Tb[:, slot(r, x), :]) for r in to_fw], m_fw, S.fw),
-        xfer(M, [(r, T.Tb[:, slot(r, x), :]) for r in to_h1], m_h1, S.h1),
+        xfer(M, [(r, T.Tb[:, slot(r, x), :]) for r in to_h1], m_all, S.h1),
         xfer(M, [(peer, T.Tb[:, slot(peer, x), :])], m_peer, S.h1),
     ], local_sem=S.sent)
-    sent = 2 * h + npeer
-    fw_total = h * len(forwards(x))
-    h1_total = h * len([q for q in direct if q not in forwards(x)]) + npeer
+    sent += 2 * nlow + npeer
+    fw_total = nlow * len(forwards(x))
+    h1_total = nlow * len([q for q in direct if q not in forwards(x)]) + npeer
 
     g.wait_ge(S.fw, fw_total)
     for y in range(n):
         if relay(y) == x:
             k0, j0, m = min(slot(x, q) for q in far(y)), min(slot(y, q) for q in far(y)), len(far(y))
             g.remote_dma_fused([xfer(T.Tb[:, k0:k0 + m, :], [(y, T.Tb[:, j0:j0 + m, :])], m_all, S.h2)], local_sem=S.sent)
-            sent += 2 * h
-    h2_total = 2 * h
+            sent += nlow
+    h2_total = nlow
 
     V.tensor_tensor(T.Tb[:, n, 0:4], T.Tt[:, 0:4], T.PR[:, 0:4], ADD).then_inc(S.sC, 1)
     V.tensor_scalar(T.Y8[:, :], T.DY[:, :], 0.125, None, MUL).then_inc(S.sY8, 1)
@@ -133,10 +142,18 @@ def rank_program(g, core, T, topo):
     V.tensor_tensor(T.YB[:, 2:4], T.Y8[:, 62:64], T.Up[:, 66:68], ADD).then_inc(S.sYB, 1)
     V.tensor_tensor(T.Y[:, 2:62], T.Y8[:, 2:62], T.Up[:, 6:66], ADD).then_inc(S.sY, 1)
     SC.wait_ge(S.sYB, 2)
-    SC.wait_ge(S.h1, h1_total)
-    SC.wait_ge(S.fw, fw_total)
-    for c, src, k in ((0, T.Tb[:, n - 1, 6:7], 0), (1, T.Tb[:, n - 1, 7:8], 1), (62, T.Tb[:, 1, 0:1], 2), (63, T.Tb[:, 1, 1:2], 3)):
-        SC.activation(T.Y[:, c:c + 1], src, ACT.Identity, bias=T.YB[:, k:k + 1], scale=0.125).then_inc(S.sY, 1)
+    SC.wait_ge(S.hl, hl_total)
+
+    def edge(out, hb, base, sem):
+        SC.activation(out, T.HB[:, hb:hb + 1], ACT.Identity, bias=base, scale=0.125).then_inc(sem, 1)
+
+    edge(T.YC[:, 0:1], 0, T.YB[:, 0:1], S.sYC)
+    edge(T.YC[:, 1:2], 3, T.YB[:, 3:4], S.sYC)
+    edge(T.Y[:, 1:2], 1, T.YB[:, 1:2], S.sY)
+    edge(T.Y[:, 62:63], 2, T.YB[:, 2:3], S.sY)
+    SC.wait_ge(S.sYC, 2)
+    edge(T.Y[:, 0:1], 1, T.YC[:, 0:1], S.sY)
+    edge(T.Y[:, 63:64], 2, T.YC[:, 1:2], S.sY)
     SY.wait_ge(S.sY, 5)
     SY.dma_start(out=T.y[:, :], in_=T.Y[:, :]).then_inc(S.st, 16)
 

from concourse.bass import DstId, RemoteDMATransfer
from concourse.mybir import AluOpType, AxisListType, ActivationFunctionType

F = "float32"
W = 12
SCRATCH = {
    "Up": ("sbuf", [128, 72], F), "Bb": ("sbuf", [128, 64], F), "B4": ("sbuf", [128, 64], F),
    "A": ("sbuf", [128, 72], F), "Tt": ("sbuf", [128, 68], F), "DY": ("sbuf", [128, 64], F),
    "Tb": ("sbuf", [128, 9, W], F), "SQ": ("sbuf", [128, 64], F), "SQ2": ("sbuf", [128, 32], F),
    "Y8": ("sbuf", [128, 64], F), "Y": ("sbuf", [128, 64], F), "YB": ("sbuf", [128, 4], F), "YC": ("sbuf", [128, 4], F),
    "HB": ("sbuf", [128, 4], F),
    "EE": ("sbuf", [128, 32], F), "PP": ("sbuf", [128, 4], F), "CS": ("sbuf", [128, 4], F), "CM": ("sbuf", [128, 4], F),
    "SO": ("sbuf", [128, 4], F),
    "PU": ("psum", [128, 512], F), "PR": ("psum", [128, 512], F),
}
SEMAPHORES = ["ldu", "ldb", "ms", "su", "sA", "sR", "sT", "sD", "sM", "sX", "sQ", "sC", "sY8", "sY", "sYB", "sYC",
              "sE", "sP", "sFm", "sFs", "sS", "hl", "h1", "fw", "h2", "sent", "st"]


def _bits(m):
    return [1 << i for i in range(m.bit_length()) if (m >> i) & 1]


def _plan(T, topo):
    cores = list(T.cores)
    n = len(cores)

    def on_chip(a, b):
        return topo.host(cores[a]) == topo.host(cores[b]) and topo.chip(cores[a]) == topo.chip(cores[b])

    def far(y):
        return [q for q in range(n) if q != y and not topo.may_write(cores[q], cores[y])]

    def relay(y):
        c = [z for z in range(n) if z != y and not on_chip(z, y) and topo.may_write(cores[z], cores[y])
             and topo.die(cores[z]) == topo.die(cores[y]) and all(topo.may_write(cores[q], cores[z]) for q in far(y))]
        return min(c, key=lambda z: (z - y) % n)

    return cores, n, on_chip, far, relay


def rank_program(g, core, T, topo):
    x = T.rank_of(core)
    if x is None:
        return
    cores, n, on_chip, far, relay = _plan(T, topo)
    S, V, SC, SY = T.sem, g.vector, g.scalar, g.sync
    ADD, SUB, MUL, MAX = AluOpType.add, AluOpType.subtract, AluOpType.mult, AluOpType.max
    AX, ACT = AxisListType.X, ActivationFunctionType

    def dst_id(r):
        rid, pid = topo.addr(cores[r], core)
        return DstId(rid=rid, pnc=pid)

    def forwards(z):
        return [q for y in range(n) if relay(y) == z for q in far(y)]

    def xfer(src, dsts, mask, sem):
        return RemoteDMATransfer(dst_ids=[dst_id(r) for r, _ in dsts], dma_engine_mask=mask, remote_sem=sem,
                                 srcs=[src], dsts=[ap for _, ap in dsts], alu_op=0)

    peer = [r for r in range(n) if r != x and on_chip(r, x)][0]
    direct = [r for r in range(n) if r != x and r != peer and topo.may_write(core, cores[r])]
    low = _bits(topo.mask(core, cores[direct[0]]))
    high = [e for e in _bits(topo.mask(core, cores[peer])) if e not in low]
    nlow, npeer = len(low), 2
    m_peer, m_all = sum(high[:npeer]), sum(low)

    SY.dma_start(out=T.Up[:, 4:68], in_=T.u[:, :]).then_inc(S.ldu, 16)
    SC.dma_start(out=T.Bb[:, :], in_=T.b[:, :]).then_inc(S.ldb, 16)

    left, right = (x - 1) % n, (x + 1) % n
    g.wait_ge(S.ldu, 16)
    g.remote_dma_fused([
        xfer(T.Up[:, 4:6], [(left, T.HB[:, 2:4])], m_peer if left == peer else m_all, S.hl),
        xfer(T.Up[:, 66:68], [(right, T.HB[:, 0:2])], m_peer if right == peer else m_all, S.hl),
    ], local_sem=S.sent)
    sent = nlow + npeer
    hl_total = nlow + npeer

    U8 = T.PU[:, 0:64]
    M = T.Tb[:, 0, :]

    V.memset(T.Up[:, 0:4], 0.0).then_inc(S.ms, 1)
    V.memset(T.Up[:, 68:72], 0.0).then_inc(S.ms, 1)
    V.memset(T.PR[:, 0:2], 0.0).then_inc(S.ms, 1)
    V.memset(T.PR[:, 66:68], 0.0).then_inc(S.ms, 1)
    V.memset(T.Tb[:, 0, 10:12], 0.0).then_inc(S.ms, 1)

    SC.wait_ge(S.ldu, 16)
    SC.activation(U8, T.Up[:, 4:68], ACT.Copy, scale=8.0).then_inc(S.su, 1)
    SC.wait_ge(S.ldb, 16)
    SC.activation(T.B4[:, :], T.Bb[:, :], ACT.Copy, scale=4.0).then_inc(S.su, 1)

    V.wait_ge(S.ms, 5)
    V.wait_ge(S.ldu, 16)
    V.tensor_tensor(T.A[:, 0:71], T.Up[:, 0:71], T.Up[:, 1:72], ADD).then_inc(S.sA, 1)
    V.wait_ge(S.su, 2)
    V.tensor_tensor(T.PR[:, 2:66], T.B4[:, :], U8, SUB).then_inc(S.sR, 1)
    V.wait_ge(S.sA, 1)
    V.tensor_tensor(T.Tt[:, :], T.A[:, 0:68], T.A[:, 3:71], ADD).then_inc(S.sT, 1)
    V.wait_ge(S.sT, 1)
    V.wait_ge(S.sR, 1)
    V.tensor_tensor(T.DY[:, :], T.Tt[:, 2:66], T.PR[:, 2:66], ADD).then_inc(S.sD, 1)
    V.tensor_tensor(T.Tb[:, 0, 0:4], T.Tt[:, 0:4], T.PR[:, 0:4], ADD).then_inc(S.sM, 1)
    V.tensor_tensor(T.Tb[:, 0, 4:8], T.Tt[:, 64:68], T.PR[:, 64:68], ADD).then_inc(S.sM, 1)
    V.wait_ge(S.sD, 1)
    V.tensor_reduce(T.Tb[:, 0, 9:10], T.DY[:, 2:62], AX, MAX, apply_absolute_value=True).then_inc(S.sX, 1)
    SC.wait_ge(S.sD, 1)
    SC.activation(T.SQ[:, 0:60], T.DY[:, 2:62], ACT.Square, scale=0.125, accum_out=T.Tb[:, 0, 8:9]).then_inc(S.sQ, 1)

    def slot(r, q):
        return (q - r) % n

    to_fw = [r for r in direct if x in forwards(r)]
    to_h1 = [r for r in direct if x not in forwards(r)]
    g.wait_ge(S.ms, 5)
    g.wait_ge(S.sM, 2)
    g.wait_ge(S.sX, 1)
    g.wait_ge(S.sQ, 1)
    g.remote_dma_fused([xfer(M, [(r, T.Tb[:, slot(r, x), :]) for r in to_fw], m_all, S.fw)], local_sem=S.sent)
    g.remote_dma_fused([
        xfer(M, [(r, T.Tb[:, slot(r, x), :]) for r in to_h1], m_all, S.h1),
        xfer(M, [(peer, T.Tb[:, slot(peer, x), :])], m_peer, S.h1),
    ], local_sem=S.sent)
    sent += 2 * nlow + npeer
    fw_total = nlow * len(forwards(x))
    h1_total = nlow * len([q for q in direct if q not in forwards(x)]) + npeer

    g.wait_ge(S.fw, fw_total)
    for y in range(n):
        if relay(y) == x:
            k0, j0, m = min(slot(x, q) for q in far(y)), min(slot(y, q) for q in far(y)), len(far(y))
            g.remote_dma_fused([xfer(T.Tb[:, k0:k0 + m, :], [(y, T.Tb[:, j0:j0 + m, :])], m_all, S.h2)], local_sem=S.sent)
            sent += nlow
    h2_total = nlow

    V.tensor_tensor(T.Tb[:, n, 0:4], T.Tt[:, 0:4], T.PR[:, 0:4], ADD).then_inc(S.sC, 1)
    V.tensor_scalar(T.Y8[:, :], T.DY[:, :], 0.125, None, MUL).then_inc(S.sY8, 1)
    V.wait_ge(S.sY8, 1)
    V.tensor_tensor(T.YB[:, 0:2], T.Y8[:, 0:2], T.Up[:, 4:6], ADD).then_inc(S.sYB, 1)
    V.tensor_tensor(T.YB[:, 2:4], T.Y8[:, 62:64], T.Up[:, 66:68], ADD).then_inc(S.sYB, 1)
    V.tensor_tensor(T.Y[:, 2:62], T.Y8[:, 2:62], T.Up[:, 6:66], ADD).then_inc(S.sY, 1)
    SC.wait_ge(S.sYB, 2)
    SC.wait_ge(S.hl, hl_total)

    def edge(out, hb, base, sem):
        SC.activation(out, T.HB[:, hb:hb + 1], ACT.Identity, bias=base, scale=0.125).then_inc(sem, 1)

    edge(T.YC[:, 0:1], 0, T.YB[:, 0:1], S.sYC)
    edge(T.YC[:, 1:2], 3, T.YB[:, 3:4], S.sYC)
    edge(T.Y[:, 1:2], 1, T.YB[:, 1:2], S.sY)
    edge(T.Y[:, 62:63], 2, T.YB[:, 2:3], S.sY)
    SC.wait_ge(S.sYC, 2)
    edge(T.Y[:, 0:1], 1, T.YC[:, 0:1], S.sY)
    edge(T.Y[:, 63:64], 2, T.YC[:, 1:2], S.sY)
    SY.wait_ge(S.sY, 5)
    SY.dma_start(out=T.y[:, :], in_=T.Y[:, :]).then_inc(S.st, 16)

    V.wait_ge(S.sM, 2)
    V.wait_ge(S.sX, 1)
    V.wait_ge(S.sQ, 1)
    V.wait_ge(S.sC, 1)
    V.wait_ge(S.h1, h1_total)
    V.wait_ge(S.fw, fw_total)
    V.wait_ge(S.h2, h2_total)
    V.tensor_tensor(T.EE[:, :], T.Tb[:, 0:n, 4:8], T.Tb[:, 1:n + 1, 0:4], ADD).then_inc(S.sE, 1)
    V.tensor_reduce(T.PP[:, 1:2], T.Tb[:, 0:n, 9], AX, MAX).then_inc(S.sP, 1)
    V.tensor_reduce(T.PP[:, 0:1], T.Tb[:, 0:n, 8], AX, ADD).then_inc(S.sP, 1)
    V.wait_ge(S.sE, 1)
    V.tensor_reduce(T.CM[:, 0:1], T.EE[:, :], AX, MAX, apply_absolute_value=True).then_inc(S.sFm, 1)
    SC.wait_ge(S.sE, 1)
    SC.activation(T.SQ2[:, :], T.EE[:, :], ACT.Square, scale=0.125, accum_out=T.CS[:, 0:1]).then_inc(S.sFs, 1)
    V.wait_ge(S.sP, 2)
    V.wait_ge(S.sFs, 1)
    V.tensor_scalar(T.SO[:, 0:1], T.CS[:, 0:1], T.PP[:, 0:1], 1.0 / 512.0, ADD, MUL).then_inc(S.sS, 1)
    V.wait_ge(S.sFm, 1)
    V.tensor_scalar(T.SO[:, 1:2], T.CM[:, 0:1], T.PP[:, 1:2], 0.125, MAX, MUL).then_inc(S.sS, 1)
    SY.wait_ge(S.sS, 2)
    SY.dma_start(out=T.s[:, :], in_=T.SO[:, 0:2]).then_inc(S.st, 16)
    g.wait_ge(S.sent, sent)
    g.wait_ge(S.h1, h1_total)
    g.wait_ge(S.h2, h2_total)
    g.wait_ge(S.st, 32)
